import numpy as np
import ml_dtypes


def mxq(x, axis, fmt="e4m3"):
    dtype, down = {"e4m3": (ml_dtypes.float8_e4m3fn, 7), "e5m2": (ml_dtypes.float8_e5m2, 14)}[fmt]
    v = np.moveaxis(np.asarray(x, np.float32).astype(ml_dtypes.bfloat16).astype(np.float64), axis, -1)
    blocks = v.reshape(v.shape[:-1] + (-1, 32))
    amax = np.abs(blocks).max(-1, keepdims=True)
    byte = np.maximum(np.where(amax > 0, np.frexp(amax)[1] - 1 + 127, 0) - down, 1)
    scale = np.exp2(byte - 127.0)
    codes = (blocks / scale).astype(np.float32).astype(dtype).astype(np.float64)
    return np.moveaxis((codes * scale).reshape(v.shape), -1, axis)


WIDE = False


def mx_kscale(k):
    if not WIDE:
        return np.ones(k)
    levels = np.array([10, -10, 5, -5, 0])
    if k % 512:
        return np.exp2(np.random.permutation(np.resize(levels, k // 32))).repeat(32)
    a = np.empty((k // 512, 16))
    for p in range(k // 512):
        a[p, :8] = np.random.permutation(np.resize(levels, 8))
        for g in range(8):
            far = levels[np.abs(levels - a[p, g]) >= 10]
            a[p, g + 8] = far[np.random.randint(len(far))]
    return np.exp2(a.ravel()).repeat(32)


def f64(x):
    return np.asarray(x).astype(np.float64)


def striped(idx):
    return np.tile(idx.reshape(-1, 16).T, (8, 1)).astype(np.uint16)


def unstriped(offs):
    return offs[:16].T.reshape(-1).astype(np.int64)


E2M1 = np.array([0.0, 0.5, 1.0, 1.5, 2.0, 3.0, 4.0, 6.0, -0.0, -0.5, -1.0, -1.5, -2.0, -3.0, -4.0, -6.0])


def pack_weight(w, fmt):
    k, n = w.shape
    w = f64(np.asarray(w, np.float32).astype(ml_dtypes.bfloat16)).reshape(k // 32, 32, n)
    amax = np.abs(w).max(1)
    if fmt == "e4m3":
        byte = np.frexp(amax)[1] - 1 + 127 - 7
    else:
        mant, ex = np.frexp(amax / 6.0)
        byte = np.where(mant > 0.5, ex, ex - 1) + 127
    byte = np.clip(np.where(amax > 0, byte, 1), 1, 254)
    scaled = (w * np.exp2(127.0 - byte)[:, None, :]).reshape(k, n).astype(np.float32)
    by_word = np.ascontiguousarray(scaled.reshape(k // 512, 128, 4, n).transpose(0, 1, 3, 2))
    if fmt == "e4m3":
        words = by_word.astype(ml_dtypes.float8_e4m3fn).view(np.uint8)
    else:
        c = by_word.astype(ml_dtypes.float4_e2m1fn).view(np.uint8) & 0xF
        words = (c[..., 0::2] | (c[..., 1::2] << 4)).reshape(k // 512, 128, 2 * n)
    return np.ascontiguousarray(words), np.ascontiguousarray(byte.astype(np.uint8).reshape(k // 512, 16, n))


def unpack_weight(words, scales, fmt):
    g, _, n = scales.shape
    words = np.ascontiguousarray(words).reshape(g, 128, n, -1)
    if fmt == "e4m3":
        vals = words.view(ml_dtypes.float8_e4m3fn).astype(np.float64)
    else:
        nib = np.empty((g, 128, n, 4), np.uint8)
        nib[..., 0::2] = words & 0xF
        nib[..., 1::2] = words >> 4
        vals = E2M1[nib]
    vals = vals * np.repeat(np.exp2(scales.astype(np.float64) - 127.0), 8, axis=1)[..., None]
    return vals.transpose(0, 1, 3, 2).reshape(g * 512, n)


def gelu(v):
    return 0.5 * v * (1.0 + np.tanh(np.sqrt(2.0 / np.pi) * (v + 0.044715 * v**3)))


K, T, S, H, T2, S2, T3, P = 1024, 2048, 512, 1024, 1024, 512, 2048, 512

def setup_inputs():
    n = np.random.standard_normal
    s = mx_kscale(K)[:, None]
    u = mx_kscale(H)[:, None]
    tab_words, tab_scales = pack_weight(n((K, T)) * s, "e4m3")
    tab2_words, tab2_scales = pack_weight(n((H, T3)) / np.sqrt(H) / u, "e4m3")
    w2_words, w2_scales = pack_weight(n((H, H)) / np.sqrt(H) / u, "e2m1")
    return {
        "tab_words": tab_words, "tab_scales": tab_scales,
        "tab2_words": tab2_words, "tab2_scales": tab2_scales,
        "w1": (0.53 * n((K, H)) / np.sqrt(K) / s).astype(np.float32),
        "w2_words": w2_words, "w2_scales": w2_scales,
        "gain": (np.exp(0.3 * n(H)) * u[:, 0]).astype(np.float32),
        "page0": (n((H, T2)) * u).astype(np.float32),
        "wgs": np.exp(0.3 * n((128, S))).astype(np.float32),
        "base": (n((H, T2)) * u).astype(np.float32),
        "age": np.exp(0.4 * n(S2)).astype(np.float32),
        "offs": striped(np.random.permutation(T)[:S]),
        "offs2": striped(np.random.permutation(T3)[:S2]),
        "offs3": striped(np.random.permutation(T2)[:S]),
        "pos1": striped(np.random.permutation(T2)[:P]),
        "pos2": striped(np.random.permutation(T2)[:P]),
    }

def reference(tab_words, tab_scales, tab2_words, tab2_scales, w1, w2_words, w2_scales, gain, page0, wgs, base, age, offs, offs2, offs3, pos1, pos2):
    v = unpack_weight(tab_words, tab_scales, "e4m3")[:, unstriped(offs)]
    v2 = unpack_weight(tab2_words, tab2_scales, "e4m3")[:, unstriped(offs2)]
    w2 = unpack_weight(w2_words, w2_scales, "e2m1")
    x = np.cos(mxq(f64(w1), 0, "e4m3").T @ v) * f64(gain)[:, None]
    h = x * (w2.T @ mxq(x, 0, "e4m3"))
    page = f64(page0).copy()
    page[:, unstriped(offs3)] = np.tile(f64(wgs), (H // 128, 1)) * h
    top = mxq(np.maximum(page, f64(base)), 0, "e4m3")
    e = v2.T @ top
    return (e[:, unstriped(pos1)] + e[:, unstriped(pos2)]) * f64(age)[:, None]

@@ -1,0 +1,354 @@
+from contextlib import ExitStack
+
+import concourse.mybir as mybir
+
+F32 = mybir.dt.float32
+BF16 = mybir.dt.bfloat16
+I32 = mybir.dt.int32
+U32 = mybir.dt.uint32
+U16 = mybir.dt.uint16
+U8 = mybir.dt.uint8
+FP8X4 = mybir.dt.float8_e4m3fn_x4
+FP4X4 = mybir.dt.float4_e2m1fn_x4
+ACT = mybir.ActivationFunctionType
+ALU = mybir.AluOpType
+
+P = 128
+PACK = 4
+PASS = P * PACK
+K, T, S, H, T2, S2, NP = 1024, 2048, 512, 1024, 1024, 512, 512
+HALF = S // 2
+FLOPS = 2 * K * H * S + 2 * H * H * S + 2 * H * S2 * T2
+
+
+def tile_list_crater_degradation_ranker_kernel(
+    tc, tab_words, tab_scales, tab2_words, tab2_scales, w1, w2_words, w2_scales,
+    gain, page0, wgs, base, age, offs, offs2, offs3, pos1, pos2, out,
+):
+    nc = tc.nc
+    with ExitStack() as ctx:
+        keep = ctx.enter_context(tc.tile_pool(name="keep", bufs=1))
+        psum = ctx.enter_context(tc.psum_pool(name="psum", bufs=1))
+
+        def held(shape, dtype, name, tag=None, bufs=1):
+            return keep.tile(shape, dtype, name=name, tag=tag or name, bufs=bufs, align_bytes=64)
+
+        def bank(shape, index, name):
+            return psum.tile(shape, F32, name=name, tag="bank%d" % index)
+
+        def load_list(src, name):
+            tile = held([P, S // 16], U16, name)
+            nc.sync.dma_start(tile[:], src)
+            return tile
+
+        def load_words(src, a, name):
+            tile = held([P, T], U32, name, tag="words", bufs=2)
+            nc.sync.dma_start(tile[:].bitcast(I32), src[a].rearrange("p t i -> p (t i)").bitcast(I32))
+            return tile
+
+        def load_table_scales(queue, src, tile):
+            for q in range(4):
+                queue.dma_start(
+                    tile[32 * q : 32 * q + 8, :].bitcast(I32), src[:, 4 * q : 4 * q + 4, :].bitcast(I32)
+                )
+
+        def w1_rows(a, c0, c1):
+            return w1[PASS * a : PASS * (a + 1), c0:c1].rearrange("(p i) c -> p i c", i=PACK)
+
+        tab_sc = held([P, T], U8, "tab_sc")
+        w2_sc_raw = held([P, 2, H], U8, "w2_sc_raw")
+        tab2_sc = held([P, T], U8, "tab2_sc")
+        nc.gpsimd.memset(tab_sc[:].bitcast(I32), 0)
+        nc.vector.memset(w2_sc_raw[:].rearrange("p a c -> p (a c)").bitcast(I32), 0)
+        nc.vector.memset(tab2_sc[:].bitcast(I32), 0)
+        tabw = {0: load_words(tab_words, 0, "tabw0")}
+        idx = load_list(offs, "idx")
+        load_table_scales(nc.sync, tab_scales, tab_sc)
+        tabw[1] = load_words(tab_words, 1, "tabw1")
+        w2_raw = held([P, 2, 2 * H], U8, "w2_raw")
+        nc.sync.dma_start(w2_raw[:].bitcast(I32), w2_words.rearrange("a p c -> p a c").bitcast(I32))
+        for q in range(4):
+            nc.sync.dma_start(
+                w2_sc_raw[32 * q : 32 * q + 4, :, :].bitcast(I32),
+                w2_scales[:, 4 * q : 4 * q + 4, :].rearrange("a r c -> r a c").bitcast(I32),
+            )
+        w1_raw = {}
+        for b, a in ((0, 0), (0, 1), (1, 0)):
+            w1_raw[b, a] = held([P, PACK, PASS], F32, "w1_raw%d%d" % (b, a), tag="stage%d" % (2 * b + a))
+            nc.sync.dma_start(w1_raw[b, a][:], w1_rows(a, PASS * b, PASS * (b + 1)))
+        g_sb = held([P, 2, PACK], F32, "g_sb")
+        nc.sync.dma_start(g_sb[:], gain.rearrange("(b p t) -> p b t", b=2, t=PACK))
+        w1_last = []
+        for u in range(2):
+            tile = held([P, PACK, PASS // 2], F32, "w1_last%d" % u)
+            nc.sync.dma_start(tile[:], w1_rows(1, PASS + u * (PASS // 2), PASS + (u + 1) * (PASS // 2)))
+            w1_last.append(tile)
+        wg = held([P, PACK, S], F32, "wg")
+        for q in (0, 2, 1, 3):
+            nc.sync.dma_start(wg[32 * q : 32 * q + 32, :, :], wgs.rearrange("(p t) j -> p t j", t=PACK))
+        idx3 = load_list(offs3, "idx3")
+        page = {}
+        base_sb = {}
+        for b in range(2):
+            rows = slice(PASS * b, PASS * (b + 1))
+            for t in range(PACK):
+                page[b, t] = held([P, T2], F32, "page%d%d" % (b, t))
+                nc.sync.dma_start(page[b, t][:], page0[rows, :].rearrange("(p t) n -> t p n", t=PACK)[t])
+        for b in range(2):
+            rows = slice(PASS * b, PASS * (b + 1))
+            for nh in range(2):
+                base_sb[b, nh] = held([P, PACK, PASS], F32, "base%d%d" % (b, nh), tag="stage%d" % (3 - 2 * b - nh))
+                nc.sync.dma_start(
+                    base_sb[b, nh][:],
+                    base[rows, PASS * nh : PASS * (nh + 1)].rearrange("(p t) n -> p t n", t=PACK),
+                )
+        load_table_scales(nc.sync, tab2_scales, tab2_sc)
+        idx2 = load_list(offs2, "idx2")
+        tab2w = [load_words(tab2_words, a, "tab2w%d" % a) for a in range(2)]
+        p1 = load_list(pos1, "p1")
+        p2 = load_list(pos2, "p2")
+        age_sb = held([P, S2 // P], F32, "age_sb")
+        with nc.allow_non_contiguous_dma(reason="one age value per partition and tile"):
+            nc.sync.dma_start(age_sb[:], age.rearrange("(m p) -> p m", p=P))
+
+        v_w = [held([P, S], U32, "v_w%d" % a) for a in range(2)]
+        v_sc = held([P, S], U8, "v_sc")
+        nc.vector.tensor_copy(v_w[0][:], tabw[0][:].indirect(idx[:]))
+        nc.vector.tensor_copy(v_sc[:], tab_sc[:].indirect(idx[:]))
+        nc.vector.tensor_copy(v_w[1][:], tabw[1][:].indirect(idx[:]))
+        m2g = held([P, 2, PACK], F32, "m2g")
+        nc.vector.tensor_scalar(m2g[:], g_sb[:], -2.0, None, ALU.mult)
+
+        w1_q = {}
+        w1_sc = {}
+
+        def deal_w1(copy, dst, raw, m0, m1):
+            copy(
+                dst[:, :, m0:m1, :].rearrange("p t m i -> p m i t"),
+                raw[:].rearrange("p i (m t) -> p m i t", t=PACK),
+            )
+
+        def quantise_w1(b, a):
+            dealt = held([P, PACK, P, PACK], BF16, "w1_bf%d%d" % (b, a), tag="w1_bf", bufs=2)
+            w1_q[b, a] = held([P, PASS], U32, "w1_q%d%d" % (b, a))
+            w1_sc[b, a] = held([P, PASS], U8, "w1_sc%d%d" % (b, a))
+            if (b, a) == (1, 1):
+                for u in range(2):
+                    deal_w1(nc.vector.tensor_copy, dealt, w1_last[u], u * (P // 2), (u + 1) * (P // 2))
+                for t in range(PACK):
+                    cols = slice(P * t, P * (t + 1))
+                    nc.vector.quantize_mx(
+                        w1_q[b, a][:, cols].bitcast(FP8X4), w1_sc[b, a][:, cols],
+                        dealt[:, t, :, :].rearrange("p m i -> p (m i)"),
+                    )
+            else:
+                deal_w1(nc.scalar.copy if (b, a) == (0, 0) else nc.vector.tensor_copy, dealt, w1_raw[b, a], 0, P)
+                nc.vector.quantize_mx(
+                    w1_q[b, a][:].bitcast(FP8X4), w1_sc[b, a][:], dealt[:].rearrange("p t m i -> p (t m i)")
+                )
+
+        z = {}
+
+        def first_product(h, b):
+            cols = slice(HALF * h, HALF * (h + 1))
+            for u in range(2):
+                z[h, b, u] = bank([P, 2, HALF], 2 * ((h + b) % 2) + u, "z%d%d%d" % (h, b, u))
+            for a in range(2):
+                for t in range(PACK):
+                    nc.tensor.matmul_mx(
+                        z[h, b, t // 2][:, t % 2, :],
+                        lhsT=w1_q[b, a][:, P * t : P * (t + 1)].bitcast(FP8X4),
+                        lhsT_scale=w1_sc[b, a][:, P * t : P * (t + 1)],
+                        rhs=v_w[a][:, cols].bitcast(FP8X4),
+                        rhs_scale=v_sc[4 * a : P, cols],
+                        start=(a == 0 and t % 2 == 0), stop=(a == 1 and t % 2 == 1),
+                    )
+
+        x = {}
+        x_q = {}
+        x_sc = {}
+
+        def cosine(h, b):
+            x[h, b] = held([P, PACK, HALF], F32, "x%d%d" % (h, b), tag="x", bufs=4)
+            tile = x[h, b]
+            for u in range(2):
+                nc.scalar.activation(tile[:, 2 * u : 2 * u + 2, :], z[h, b, u][:], ACT.Sin, scale=0.5)
+            split = (h, b) == (0, 1)
+            for u in range(1 if split else 0, 2):
+                nc.scalar.activation(tile[:, 2 * u : 2 * u + 2, :], tile[:, 2 * u : 2 * u + 2, :], ACT.Square)
+            for t in range(PACK):
+                if split and t < 2:
+                    nc.vector.scalar_tensor_tensor(
+                        tile[:, t, :], tile[:, t, :], m2g[:, b, t : t + 1], tile[:, t, :], ALU.mult, ALU.mult
+                    )
+            for t in range(PACK):
+                if split and t < 2:
+                    nc.vector.tensor_scalar(tile[:, t, :], tile[:, t, :], g_sb[:, b, t : t + 1], None, ALU.add)
+                elif h == 0:
+                    nc.vector.tensor_scalar(
+                        tile[:, t, :], tile[:, t, :], m2g[:, b, t : t + 1], g_sb[:, b, t : t + 1], ALU.mult, ALU.add
+                    )
+                else:
+                    nc.scalar.activation(
+                        tile[:, t, :], tile[:, t, :], ACT.Identity,
+                        bias=g_sb[:, b, t : t + 1], scale=m2g[:, b, t : t + 1],
+                    )
+            x_bf = held([P, HALF, PACK], BF16, "x_bf%d%d" % (h, b), tag="mid" if (h, b) == (1, 1) else None)
+            copy = nc.vector.tensor_copy if h == 0 else nc.scalar.copy
+            copy(
+                x_bf[:].rearrange("p (c i) t -> p c t i", i=4),
+                tile[:].rearrange("p t (c i) -> p c t i", i=4),
+            )
+            x_q[h, b] = held([P, HALF], U32, "x_q%d%d" % (h, b))
+            x_sc[h, b] = held([P, HALF], U8, "x_sc%d%d" % (h, b))
+            nc.vector.quantize_mx(
+                x_q[h, b][:].bitcast(FP8X4), x_sc[h, b][:], x_bf[:].rearrange("p j t -> p (j t)")
+            )
+
+        w2_q = held([P, 4, PACK, P], U16, "w2_q")
+        w2_sc = held([P, 4, PACK, P], U8, "w2_sc")
+
+        def deal_w2():
+            nc.vector.tensor_copy(
+                w2_sc[:].rearrange("p g t m -> p g m t"),
+                w2_sc_raw[:].rearrange("p a (b m t) -> p (a b) m t", b=2, t=PACK),
+            )
+            nc.vector.tensor_copy(
+                w2_q[:].rearrange("p g t m -> p g m t"),
+                w2_raw[:].rearrange("p a c -> p (a c)").bitcast(U16).rearrange("p (g m t) -> p g m t", g=4, t=PACK),
+            )
+
+        y = {}
+
+        def second_product(h):
+            acc = {}
+            for b in range(2):
+                y[h, b] = held([P, PACK, HALF], F32, "y%d%d" % (h, b), tag="y", bufs=4)
+                for u in range(2):
+                    acc[b, u] = bank([P, 2, HALF], 4 * (1 - h) + 2 * b + u, "y_ps%d%d%d" % (h, b, u))
+            for a in range(2):
+                for b in range(2):
+                    for t in range(PACK):
+                        nc.tensor.matmul_mx(
+                            acc[b, t // 2][:, t % 2, :],
+                            lhsT=w2_q[:, 2 * a + b, t, :].bitcast(FP4X4),
+                            lhsT_scale=w2_sc[:, 2 * a + b, t, :],
+                            rhs=x_q[h, a][:].bitcast(FP8X4),
+                            rhs_scale=x_sc[h, a][:],
+                            start=(a == 0 and t % 2 == 0), stop=(a == 1 and t % 2 == 1),
+                        )
+            for b in range(2):
+                for u in range(2):
+                    nc.scalar.copy(y[h, b][:, 2 * u : 2 * u + 2, :], acc[b, u][:])
+
+        def place(h, b):
+            for u in range(2):
+                if (h, b, u) == (0, 1, 1):
+                    xw = held([P, 2, HALF], F32, "xw_mid", tag="mid")
+                elif (h, b) == (1, 1):
+                    xw = held([P, 2, HALF], F32, "xw_end%d" % u, tag="stage%d" % (2 + u))
+                else:
+                    xw = held([P, 2, HALF], F32, "xw%d%d%d" % (h, b, u), tag="xw", bufs=5)
+                nc.vector.tensor_tensor(
+                    xw[:], x[h, b][:, 2 * u : 2 * u + 2, :], wg[:, 2 * u : 2 * u + 2, HALF * h : HALF * (h + 1)], ALU.mult
+                )
+                for e in range(2):
+                    t = 2 * u + e
+                    nc.vector.tensor_tensor(
+                        page[b, t][:].indirect(idx3[:, 16 * h : 16 * (h + 1)]), xw[:, e, :], y[h, b][:, t, :], ALU.mult
+                    )
+
+        top_q = {}
+        top_sc = {}
+
+        def raise_to_base(b):
+            top_q[b] = held([P, T2], U32, "top_q%d" % b)
+            top_sc[b] = held([P, T2], U8, "top_sc%d" % b)
+            parts = 1 if b == 0 else 2
+            width = PASS // parts
+            for nh in range(2):
+                top = held([P, PACK, PASS], BF16, "top%d%d" % (b, nh), tag="top", bufs=4)
+                for t in range(PACK):
+                    nc.vector.tensor_tensor(
+                        top[:, t, :], page[b, t][:, PASS * nh : PASS * (nh + 1)], base_sb[b, nh][:, t, :], ALU.max
+                    )
+                for part in range(parts):
+                    if (b, nh, part) == (1, 1, 1):
+                        woven = held([P, width, PACK], BF16, "woven_last", tag="late")
+                    else:
+                        woven = held([P, width, PACK], BF16, "woven%d%d%d" % (b, nh, part), tag="x", bufs=4)
+                    nc.scalar.copy(
+                        woven[:].rearrange("p (c i) t -> p c t i", i=4),
+                        top[:, :, width * part : width * (part + 1)].rearrange("p t (c i) -> p c t i", i=4),
+                    )
+                    cols = slice(PASS * nh + width * part, PASS * nh + width * (part + 1))
+                    nc.vector.quantize_mx(
+                        top_q[b][:, cols].bitcast(FP8X4), top_sc[b][:, cols], woven[:].rearrange("p n t -> p (n t)")
+                    )
+
+        def candidates(mh):
+            words = held([P, 2, HALF], U32, "v2_w%d" % mh, tag="late" if mh == 1 else None)
+            scales = held([P, HALF], U8, "v2_sc%d" % mh)
+            entries = idx2[:, 16 * mh : 16 * (mh + 1)]
+            nc.vector.tensor_copy(scales[:], tab2_sc[:].indirect(entries))
+            for a in range(2):
+                nc.vector.tensor_copy(words[:, a, :], tab2w[a][:].indirect(entries))
+            return words, scales
+
+        def scores(m, words, scales):
+            cols = slice(P * (m % 2), P * (m % 2 + 1))
+            e_sb = held([P, T2], F32, "e%d" % m, tag="y", bufs=4)
+            for nh in range(2):
+                acc = bank([P, PASS], (2 * m + nh + 4) % 8, "e_ps%d%d" % (m, nh))
+                n_cols = slice(PASS * nh, PASS * (nh + 1))
+                for a in range(2):
+                    nc.tensor.matmul_mx(
+                        acc[:],
+                        lhsT=words[:, a, cols].bitcast(FP8X4), lhsT_scale=scales[4 * a : P, cols],
+                        rhs=top_q[a][:, n_cols].bitcast(FP8X4), rhs_scale=top_sc[a][:, n_cols],
+                        start=(a == 0), stop=(a == 1),
+                    )
+                nc.scalar.copy(e_sb[:, n_cols], acc[:])
+            return e_sb
+
+        def pairs(m, e_sb):
+            picked = held([P, 2, NP], F32, "picked%d" % m, tag="top", bufs=4)
+            parts = 2 if m == 3 else 1
+            width = NP // parts
+            for part in range(parts):
+                cols = slice(width * part, width * (part + 1))
+                entries = slice(width // 16 * part, width // 16 * (part + 1))
+                nc.vector.tensor_copy(picked[:, 0, cols], e_sb[:].indirect(p1[:, entries]))
+                nc.vector.tensor_tensor(
+                    picked[:, 1, cols], e_sb[:].indirect(p2[:, entries]), picked[:, 0, cols], ALU.add
+                )
+                nc.scalar.activation(picked[:, 0, cols], picked[:, 1, cols], ACT.Copy, scale=age_sb[:, m : m + 1])
+                nc.sync.dma_start(out[P * m : P * (m + 1), cols], picked[:, 0, cols])
+
+        deal_w2()
+        quantise_w1(0, 0)
+        quantise_w1(0, 1)
+        first_product(0, 0)
+        quantise_w1(1, 0)
+        quantise_w1(1, 1)
+        cosine(0, 0)
+        first_product(0, 1)
+        cosine(0, 1)
+        second_product(0)
+        first_product(1, 0)
+        first_product(1, 1)
+        cosine(1, 0)
+        cosine(1, 1)
+        second_product(1)
+        place(0, 0)
+        place(0, 1)
+        place(1, 0)
+        raise_to_base(0)
+        place(1, 1)
+        raise_to_base(1)
+        first = candidates(0)
+        e_low = [scores(m, *first) for m in range(2)]
+        second = candidates(1)
+        e_high = [scores(m, *second) for m in range(2, 4)]
+        for m, e_sb in enumerate(e_low + e_high):
+            pairs(m, e_sb)

@@ -41,9 +41,12 @@ def tile_list_crater_degradation_ranker_kernel(
             nc.sync.dma_start(tile[:], src)
             return tile
 
-        def load_words(src, a, name):
+        def load_words(src, a, name, parts=1):
             tile = held([P, T], U32, name, tag="words", bufs=2)
-            nc.sync.dma_start(tile[:].bitcast(I32), src[a].rearrange("p t i -> p (t i)").bitcast(I32))
+            rows = src[a].rearrange("p t i -> p (t i)").bitcast(I32)
+            for part in range(parts):
+                cols = slice(T // parts * part, T // parts * (part + 1))
+                nc.sync.dma_start(tile[:, cols].bitcast(I32), rows[:, cols])
             return tile
 
         def load_table_scales(queue, src, tile):
@@ -58,26 +61,31 @@ def tile_list_crater_degradation_ranker_kernel(
         tab_sc = held([P, T], U8, "tab_sc")
         w2_sc_raw = held([P, 2, H], U8, "w2_sc_raw")
         tab2_sc = held([P, T], U8, "tab2_sc")
-        nc.gpsimd.memset(tab_sc[:].bitcast(I32), 0)
+        nc.vector.memset(tab_sc[:].bitcast(I32), 0)
         nc.vector.memset(w2_sc_raw[:].rearrange("p a c -> p (a c)").bitcast(I32), 0)
         nc.vector.memset(tab2_sc[:].bitcast(I32), 0)
-        tabw = {0: load_words(tab_words, 0, "tabw0")}
+        w1_raw = {}
+
+        def load_w1(b, a):
+            w1_raw[b, a] = held([P, PACK, PASS], F32, "w1_raw%d%d" % (b, a), tag="stage%d" % (2 * b + a))
+            nc.sync.dma_start(w1_raw[b, a][:], w1_rows(a, PASS * b, PASS * (b + 1)))
+
+        tabw = {0: load_words(tab_words, 0, "tabw0", parts=2)}
         idx = load_list(offs, "idx")
+        load_w1(0, 0)
         load_table_scales(nc.sync, tab_scales, tab_sc)
         tabw[1] = load_words(tab_words, 1, "tabw1")
         w2_raw = held([P, 2, 2 * H], U8, "w2_raw")
         nc.sync.dma_start(w2_raw[:].bitcast(I32), w2_words.rearrange("a p c -> p a c").bitcast(I32))
+        g_sb = held([P, 2, PACK], F32, "g_sb")
+        nc.sync.dma_start(g_sb[:], gain.rearrange("(b p t) -> p b t", b=2, t=PACK))
         for q in range(4):
             nc.sync.dma_start(
                 w2_sc_raw[32 * q : 32 * q + 4, :, :].bitcast(I32),
                 w2_scales[:, 4 * q : 4 * q + 4, :].rearrange("a r c -> r a c").bitcast(I32),
             )
-        w1_raw = {}
-        for b, a in ((0, 0), (0, 1), (1, 0)):
-            w1_raw[b, a] = held([P, PACK, PASS], F32, "w1_raw%d%d" % (b, a), tag="stage%d" % (2 * b + a))
-            nc.sync.dma_start(w1_raw[b, a][:], w1_rows(a, PASS * b, PASS * (b + 1)))
-        g_sb = held([P, 2, PACK], F32, "g_sb")
-        nc.sync.dma_start(g_sb[:], gain.rearrange("(b p t) -> p b t", b=2, t=PACK))
+        load_w1(0, 1)
+        load_w1(1, 0)
         w1_last = []
         for u in range(2):
             tile = held([P, PACK, PASS // 2], F32, "w1_last%d" % u)
@@ -94,14 +102,13 @@ def tile_list_crater_degradation_ranker_kernel(
             for t in range(PACK):
                 page[b, t] = held([P, T2], F32, "page%d%d" % (b, t))
                 nc.sync.dma_start(page[b, t][:], page0[rows, :].rearrange("(p t) n -> t p n", t=PACK)[t])
-        for b in range(2):
-            rows = slice(PASS * b, PASS * (b + 1))
-            for nh in range(2):
-                base_sb[b, nh] = held([P, PACK, PASS], F32, "base%d%d" % (b, nh), tag="stage%d" % (3 - 2 * b - nh))
-                nc.sync.dma_start(
-                    base_sb[b, nh][:],
-                    base[rows, PASS * nh : PASS * (nh + 1)].rearrange("(p t) n -> p t n", t=PACK),
-                )
+        base_rows = [base[PASS * b : PASS * (b + 1), :].rearrange("(p t) n -> p t n", t=PACK) for b in range(2)]
+        for u in range(2):
+            base_sb[0, u] = held([P, 2, T2], F32, "base0%d" % u, tag="stage%d" % (3 - u))
+            nc.sync.dma_start(base_sb[0, u][:], base_rows[0][:, 2 * u : 2 * u + 2, :])
+        for nh in range(2):
+            base_sb[1, nh] = held([P, PACK, PASS], F32, "base1%d" % nh, tag="stage%d" % (1 - nh))
+            nc.sync.dma_start(base_sb[1, nh][:], base_rows[1][:, :, PASS * nh : PASS * (nh + 1)])
         load_table_scales(nc.sync, tab2_scales, tab2_sc)
         idx2 = load_list(offs2, "idx2")
         tab2w = [load_words(tab2_words, a, "tab2w%d" % a) for a in range(2)]
@@ -152,7 +159,7 @@ def tile_list_crater_degradation_ranker_kernel(
         def first_product(h, b):
             cols = slice(HALF * h, HALF * (h + 1))
             for u in range(2):
-                z[h, b, u] = bank([P, 2, HALF], 2 * ((h + b) % 2) + u, "z%d%d%d" % (h, b, u))
+                z[h, b, u] = bank([P, 2, HALF], 2 * (h + b) + u, "z%d%d%d" % (h, b, u))
             for a in range(2):
                 for t in range(PACK):
                     nc.tensor.matmul_mx(
@@ -169,13 +176,18 @@ def tile_list_crater_degradation_ranker_kernel(
         x_sc = {}
 
         def cosine(h, b):
-            x[h, b] = held([P, PACK, HALF], F32, "x%d%d" % (h, b), tag="x", bufs=4)
-            tile = x[h, b]
+            if (h, b) == (1, 0):
+                sines = held([P, PACK, HALF], F32, "sines10", tag="x", bufs=4)
+                tile = held([P, PACK, HALF], F32, "x10", tag="c2")
+            else:
+                tile = held([P, PACK, HALF], F32, "x%d%d" % (h, b), tag="x", bufs=4)
+                sines = tile
+            x[h, b] = tile
             for u in range(2):
-                nc.scalar.activation(tile[:, 2 * u : 2 * u + 2, :], z[h, b, u][:], ACT.Sin, scale=0.5)
+                nc.scalar.activation(sines[:, 2 * u : 2 * u + 2, :], z[h, b, u][:], ACT.Sin, scale=0.5)
             split = (h, b) == (0, 1)
             for u in range(1 if split else 0, 2):
-                nc.scalar.activation(tile[:, 2 * u : 2 * u + 2, :], tile[:, 2 * u : 2 * u + 2, :], ACT.Square)
+                nc.scalar.activation(tile[:, 2 * u : 2 * u + 2, :], sines[:, 2 * u : 2 * u + 2, :], ACT.Square)
             for t in range(PACK):
                 if split and t < 2:
                     nc.vector.scalar_tensor_tensor(
@@ -184,7 +196,7 @@ def tile_list_crater_degradation_ranker_kernel(
             for t in range(PACK):
                 if split and t < 2:
                     nc.vector.tensor_scalar(tile[:, t, :], tile[:, t, :], g_sb[:, b, t : t + 1], None, ALU.add)
-                elif h == 0:
+                elif split:
                     nc.vector.tensor_scalar(
                         tile[:, t, :], tile[:, t, :], m2g[:, b, t : t + 1], g_sb[:, b, t : t + 1], ALU.mult, ALU.add
                     )
@@ -193,17 +205,24 @@ def tile_list_crater_degradation_ranker_kernel(
                         tile[:, t, :], tile[:, t, :], ACT.Identity,
                         bias=g_sb[:, b, t : t + 1], scale=m2g[:, b, t : t + 1],
                     )
-            x_bf = held([P, HALF, PACK], BF16, "x_bf%d%d" % (h, b), tag="mid" if (h, b) == (1, 1) else None)
-            copy = nc.vector.tensor_copy if h == 0 else nc.scalar.copy
-            copy(
-                x_bf[:].rearrange("p (c i) t -> p c t i", i=4),
-                tile[:].rearrange("p t (c i) -> p c t i", i=4),
-            )
             x_q[h, b] = held([P, HALF], U32, "x_q%d%d" % (h, b))
             x_sc[h, b] = held([P, HALF], U8, "x_sc%d%d" % (h, b))
-            nc.vector.quantize_mx(
-                x_q[h, b][:].bitcast(FP8X4), x_sc[h, b][:], x_bf[:].rearrange("p j t -> p (j t)")
-            )
+            tags = {(0, 1): ["c1", "c2"], (1, 1): ["mid"]}.get((h, b), [None])
+            width = HALF // len(tags)
+            copy = nc.vector.tensor_copy if h == 0 else nc.scalar.copy
+            woven = []
+            for part, tag in enumerate(tags):
+                x_bf = held([P, width, PACK], BF16, "x_bf%d%d%d" % (h, b, part), tag=tag)
+                copy(
+                    x_bf[:].rearrange("p (c i) t -> p c t i", i=4),
+                    tile[:, :, width * part : width * (part + 1)].rearrange("p t (c i) -> p c t i", i=4),
+                )
+                woven.append(x_bf)
+            for part, x_bf in enumerate(woven):
+                cols = slice(width * part, width * (part + 1))
+                nc.vector.quantize_mx(
+                    x_q[h, b][:, cols].bitcast(FP8X4), x_sc[h, b][:, cols], x_bf[:].rearrange("p j t -> p (j t)")
+                )
 
         w2_q = held([P, 4, PACK, P], U16, "w2_q")
         w2_sc = held([P, 4, PACK, P], U8, "w2_sc")
@@ -242,18 +261,14 @@ def tile_list_crater_degradation_ranker_kernel(
                     nc.scalar.copy(y[h, b][:, 2 * u : 2 * u + 2, :], acc[b, u][:])
 
         def place(h, b):
-            for u in range(2):
-                if (h, b, u) == (0, 1, 1):
-                    xw = held([P, 2, HALF], F32, "xw_mid", tag="mid")
-                elif (h, b) == (1, 1):
-                    xw = held([P, 2, HALF], F32, "xw_end%d" % u, tag="stage%d" % (2 + u))
-                else:
-                    xw = held([P, 2, HALF], F32, "xw%d%d%d" % (h, b, u), tag="xw", bufs=5)
-                nc.vector.tensor_tensor(
-                    xw[:], x[h, b][:, 2 * u : 2 * u + 2, :], wg[:, 2 * u : 2 * u + 2, HALF * h : HALF * (h + 1)], ALU.mult
-                )
-                for e in range(2):
-                    t = 2 * u + e
+            tags = {(0, 0): ["c1"], (0, 1): ["c1", "mid"], (1, 0): [None], (1, 1): ["stage2"]}[h, b]
+            rows = PACK // len(tags)
+            for part, tag in enumerate(tags):
+                ts = slice(rows * part, rows * (part + 1))
+                xw = held([P, rows, HALF], F32, "xw%d%d%d" % (h, b, part), tag=tag)
+                nc.vector.tensor_tensor(xw[:], x[h, b][:, ts, :], wg[:, ts, HALF * h : HALF * (h + 1)], ALU.mult)
+                for e in range(rows):
+                    t = rows * part + e
                     nc.vector.tensor_tensor(
                         page[b, t][:].indirect(idx3[:, 16 * h : 16 * (h + 1)]), xw[:, e, :], y[h, b][:, t, :], ALU.mult
                     )
@@ -261,29 +276,39 @@ def tile_list_crater_degradation_ranker_kernel(
         top_q = {}
         top_sc = {}
 
+        def weave_and_quantise(b, top, src_cols, dst_cols, name, tag, bufs):
+            width = dst_cols.stop - dst_cols.start
+            woven = held([P, width, PACK], BF16, name, tag=tag, bufs=bufs)
+            nc.scalar.copy(
+                woven[:].rearrange("p (c i) t -> p c t i", i=4),
+                top[:, :, src_cols].rearrange("p t (c i) -> p c t i", i=4),
+            )
+            nc.vector.quantize_mx(
+                top_q[b][:, dst_cols].bitcast(FP8X4), top_sc[b][:, dst_cols], woven[:].rearrange("p n t -> p (n t)")
+            )
+
         def raise_to_base(b):
             top_q[b] = held([P, T2], U32, "top_q%d" % b)
             top_sc[b] = held([P, T2], U8, "top_sc%d" % b)
-            parts = 1 if b == 0 else 2
-            width = PASS // parts
+            if b == 0:
+                top = held([P, PACK, T2], BF16, "top0")
+                for t in range(PACK):
+                    nc.vector.tensor_tensor(top[:, t, :], page[b, t][:], base_sb[b, t // 2][:, t % 2, :], ALU.max)
+                weave_and_quantise(b, top, slice(0, T2), slice(0, T2), "woven0", None, 1)
+                return
+            width = PASS // 2
             for nh in range(2):
-                top = held([P, PACK, PASS], BF16, "top%d%d" % (b, nh), tag="top", bufs=4)
+                top = held([P, PACK, PASS], BF16, "top1%d" % nh, tag="top", bufs=2)
                 for t in range(PACK):
                     nc.vector.tensor_tensor(
                         top[:, t, :], page[b, t][:, PASS * nh : PASS * (nh + 1)], base_sb[b, nh][:, t, :], ALU.max
                     )
-                for part in range(parts):
-                    if (b, nh, part) == (1, 1, 1):
-                        woven = held([P, width, PACK], BF16, "woven_last", tag="late")
-                    else:
-                        woven = held([P, width, PACK], BF16, "woven%d%d%d" % (b, nh, part), tag="x", bufs=4)
-                    nc.scalar.copy(
-                        woven[:].rearrange("p (c i) t -> p c t i", i=4),
-                        top[:, :, width * part : width * (part + 1)].rearrange("p t (c i) -> p c t i", i=4),
-                    )
-                    cols = slice(PASS * nh + width * part, PASS * nh + width * (part + 1))
-                    nc.vector.quantize_mx(
-                        top_q[b][:, cols].bitcast(FP8X4), top_sc[b][:, cols], woven[:].rearrange("p n t -> p (n t)")
+                for part in range(2):
+                    last = (nh, part) == (1, 1)
+                    c0 = width * part
+                    weave_and_quantise(
+                        b, top, slice(c0, c0 + width), slice(PASS * nh + c0, PASS * nh + c0 + width),
+                        "woven1%d%d" % (nh, part), "late" if last else "x", 1 if last else 4,
                     )
 
         def candidates(mh):
@@ -299,7 +324,7 @@ def tile_list_crater_degradation_ranker_kernel(
             cols = slice(P * (m % 2), P * (m % 2 + 1))
             e_sb = held([P, T2], F32, "e%d" % m, tag="y", bufs=4)
             for nh in range(2):
-                acc = bank([P, PASS], (2 * m + nh + 4) % 8, "e_ps%d%d" % (m, nh))
+                acc = bank([P, PASS], (6, 4, 0, 2)[m] + nh, "e_ps%d%d" % (m, nh))
                 n_cols = slice(PASS * nh, PASS * (nh + 1))
                 for a in range(2):
                     nc.tensor.matmul_mx(
@@ -312,12 +337,11 @@ def tile_list_crater_degradation_ranker_kernel(
             return e_sb
 
         def pairs(m, e_sb):
-            picked = held([P, 2, NP], F32, "picked%d" % m, tag="top", bufs=4)
-            parts = 2 if m == 3 else 1
-            width = NP // parts
-            for part in range(parts):
-                cols = slice(width * part, width * (part + 1))
-                entries = slice(width // 16 * part, width // 16 * (part + 1))
+            picked = held([P, 2, NP], F32, "picked%d" % m, tag="top", bufs=2)
+            edges = (0, 384, NP) if m == 3 else (0, NP)
+            for c0, c1 in zip(edges[:-1], edges[1:]):
+                cols = slice(c0, c1)
+                entries = slice(c0 // 16, c1 // 16)
                 nc.vector.tensor_copy(picked[:, 0, cols], e_sb[:].indirect(p1[:, entries]))
                 nc.vector.tensor_tensor(
                     picked[:, 1, cols], e_sb[:].indirect(p2[:, entries]), picked[:, 0, cols], ALU.add
@@ -325,8 +349,8 @@ def tile_list_crater_degradation_ranker_kernel(
                 nc.scalar.activation(picked[:, 0, cols], picked[:, 1, cols], ACT.Copy, scale=age_sb[:, m : m + 1])
                 nc.sync.dma_start(out[P * m : P * (m + 1), cols], picked[:, 0, cols])
 
-        deal_w2()
         quantise_w1(0, 0)
+        deal_w2()
         quantise_w1(0, 1)
         first_product(0, 0)
         quantise_w1(1, 0)

@@ -18,6 +18,7 @@ PACK = 4
 PASS = P * PACK
 K, T, S, H, T2, S2, NP = 1024, 2048, 512, 1024, 1024, 512, 512
 HALF = S // 2
+SCALAR_SHARE = 64
 FLOPS = 2 * K * H * S + 2 * H * H * S + 2 * H * S2 * T2
 
 
@@ -72,11 +73,11 @@ def tile_list_crater_degradation_ranker_kernel(
 
         tabw = {0: load_words(tab_words, 0, "tabw0", parts=2)}
         idx = load_list(offs, "idx")
-        load_w1(0, 0)
-        load_table_scales(nc.sync, tab_scales, tab_sc)
         tabw[1] = load_words(tab_words, 1, "tabw1")
+        load_table_scales(nc.sync, tab_scales, tab_sc)
         w2_raw = held([P, 2, 2 * H], U8, "w2_raw")
         nc.sync.dma_start(w2_raw[:].bitcast(I32), w2_words.rearrange("a p c -> p a c").bitcast(I32))
+        load_w1(0, 0)
         g_sb = held([P, 2, PACK], F32, "g_sb")
         nc.sync.dma_start(g_sb[:], gain.rearrange("(b p t) -> p b t", b=2, t=PACK))
         for q in range(4):
@@ -124,7 +125,7 @@ def tile_list_crater_degradation_ranker_kernel(
         nc.vector.tensor_copy(v_sc[:], tab_sc[:].indirect(idx[:]))
         nc.vector.tensor_copy(v_w[1][:], tabw[1][:].indirect(idx[:]))
         m2g = held([P, 2, PACK], F32, "m2g")
-        nc.vector.tensor_scalar(m2g[:], g_sb[:], -2.0, None, ALU.mult)
+        nc.scalar.activation(m2g[:], g_sb[:], ACT.Copy, scale=-2.0)
 
         w1_q = {}
         w1_sc = {}
@@ -132,16 +133,16 @@ def tile_list_crater_degradation_ranker_kernel(
         def deal_w1(copy, dst, raw, m0, m1):
             copy(
                 dst[:, :, m0:m1, :].rearrange("p t m i -> p m i t"),
-                raw[:].rearrange("p i (m t) -> p m i t", t=PACK),
+                raw.rearrange("p i (m t) -> p m i t", t=PACK),
             )
 
         def quantise_w1(b, a):
-            dealt = held([P, PACK, P, PACK], BF16, "w1_bf%d%d" % (b, a), tag="w1_bf", bufs=2)
+            dealt = held([P, PACK, P, PACK], BF16, "w1_bf%d%d" % (b, a), tag="bfb" if (b, a) == (0, 1) else "bfa")
             w1_q[b, a] = held([P, PASS], U32, "w1_q%d%d" % (b, a))
             w1_sc[b, a] = held([P, PASS], U8, "w1_sc%d%d" % (b, a))
             if (b, a) == (1, 1):
                 for u in range(2):
-                    deal_w1(nc.vector.tensor_copy, dealt, w1_last[u], u * (P // 2), (u + 1) * (P // 2))
+                    deal_w1(nc.vector.tensor_copy, dealt, w1_last[u][:], u * (P // 2), (u + 1) * (P // 2))
                 for t in range(PACK):
                     cols = slice(P * t, P * (t + 1))
                     nc.vector.quantize_mx(
@@ -149,7 +150,11 @@ def tile_list_crater_degradation_ranker_kernel(
                         dealt[:, t, :, :].rearrange("p m i -> p (m i)"),
                     )
             else:
-                deal_w1(nc.scalar.copy if (b, a) == (0, 0) else nc.vector.tensor_copy, dealt, w1_raw[b, a], 0, P)
+                m_scalar = {(0, 0): P, (0, 1): SCALAR_SHARE, (1, 0): 0}[b, a]
+                if m_scalar > 0:
+                    deal_w1(nc.scalar.copy, dealt, w1_raw[b, a][:, :, : PACK * m_scalar], 0, m_scalar)
+                if m_scalar < P:
+                    deal_w1(nc.vector.tensor_copy, dealt, w1_raw[b, a][:, :, PACK * m_scalar :], m_scalar, P)
                 nc.vector.quantize_mx(
                     w1_q[b, a][:].bitcast(FP8X4), w1_sc[b, a][:], dealt[:].rearrange("p t m i -> p (t m i)")
                 )
@@ -207,7 +212,7 @@ def tile_list_crater_degradation_ranker_kernel(
                     )
             x_q[h, b] = held([P, HALF], U32, "x_q%d%d" % (h, b))
             x_sc[h, b] = held([P, HALF], U8, "x_sc%d%d" % (h, b))
-            tags = {(0, 1): ["c1", "c2"], (1, 1): ["mid"]}.get((h, b), [None])
+            tags = {(0, 0): ["bfa"], (0, 1): ["c1", "c2"], (1, 0): [None], (1, 1): ["mid"]}[h, b]
             width = HALF // len(tags)
             copy = nc.vector.tensor_copy if h == 0 else nc.scalar.copy
             woven = []
@@ -229,12 +234,12 @@ def tile_list_crater_degradation_ranker_kernel(
 
         def deal_w2():
             nc.vector.tensor_copy(
-                w2_sc[:].rearrange("p g t m -> p g m t"),
-                w2_sc_raw[:].rearrange("p a (b m t) -> p (a b) m t", b=2, t=PACK),
-            )
-            nc.vector.tensor_copy(
                 w2_q[:].rearrange("p g t m -> p g m t"),
                 w2_raw[:].rearrange("p a c -> p (a c)").bitcast(U16).rearrange("p (g m t) -> p g m t", g=4, t=PACK),
+            )
+            nc.vector.tensor_copy(
+                w2_sc[:].rearrange("p g t m -> p g m t"),
+                w2_sc_raw[:].rearrange("p a (b m t) -> p (a b) m t", b=2, t=PACK),
             )
 
         y = {}
@@ -312,8 +317,8 @@ def tile_list_crater_degradation_ranker_kernel(
                     )
 
         def candidates(mh):
-            words = held([P, 2, HALF], U32, "v2_w%d" % mh, tag="late" if mh == 1 else None)
-            scales = held([P, HALF], U8, "v2_sc%d" % mh)
+            words = held([P, 2, HALF], U32, "v2_w%d" % mh, tag="late" if mh == 1 else "stage1")
+            scales = held([P, HALF], U8, "v2_sc%d" % mh, tag="stage0" if mh == 1 else "stage2")
             entries = idx2[:, 16 * mh : 16 * (mh + 1)]
             nc.vector.tensor_copy(scales[:], tab2_sc[:].indirect(entries))
             for a in range(2):
@@ -336,21 +341,24 @@ def tile_list_crater_degradation_ranker_kernel(
                 nc.scalar.copy(e_sb[:, n_cols], acc[:])
             return e_sb
 
-        def pairs(m, e_sb):
-            picked = held([P, 2, NP], F32, "picked%d" % m, tag="top", bufs=2)
+        picked = {}
+
+        def pick_first(m, e_sb):
+            picked[m] = held([P, 2, NP], F32, "picked%d" % m, tag="x", bufs=4)
+            nc.vector.tensor_copy(picked[m][:, 0, :], e_sb[:].indirect(p1[:]))
+
+        def add_second(m, e_sb):
             edges = (0, 384, NP) if m == 3 else (0, NP)
             for c0, c1 in zip(edges[:-1], edges[1:]):
                 cols = slice(c0, c1)
-                entries = slice(c0 // 16, c1 // 16)
-                nc.vector.tensor_copy(picked[:, 0, cols], e_sb[:].indirect(p1[:, entries]))
                 nc.vector.tensor_tensor(
-                    picked[:, 1, cols], e_sb[:].indirect(p2[:, entries]), picked[:, 0, cols], ALU.add
+                    picked[m][:, 1, cols], e_sb[:].indirect(p2[:, c0 // 16 : c1 // 16]), picked[m][:, 0, cols], ALU.add
                 )
-                nc.scalar.activation(picked[:, 0, cols], picked[:, 1, cols], ACT.Copy, scale=age_sb[:, m : m + 1])
-                nc.sync.dma_start(out[P * m : P * (m + 1), cols], picked[:, 0, cols])
+                nc.scalar.activation(picked[m][:, 0, cols], picked[m][:, 1, cols], ACT.Copy, scale=age_sb[:, m : m + 1])
+                nc.sync.dma_start(out[P * m : P * (m + 1), cols], picked[m][:, 0, cols])
 
-        quantise_w1(0, 0)
         deal_w2()
+        quantise_w1(0, 0)
         quantise_w1(0, 1)
         first_product(0, 0)
         quantise_w1(1, 0)
@@ -374,5 +382,9 @@ def tile_list_crater_degradation_ranker_kernel(
         e_low = [scores(m, *first) for m in range(2)]
         second = candidates(1)
         e_high = [scores(m, *second) for m in range(2, 4)]
-        for m, e_sb in enumerate(e_low + e_high):
-            pairs(m, e_sb)
+        e_all = e_low + e_high
+        pick_first(0, e_all[0])
+        for m in range(4):
+            if m < 3:
+                pick_first(m + 1, e_all[m + 1])
+            add_second(m, e_all[m])

@@ -1,6 +1,7 @@
 from contextlib import ExitStack
 
 import concourse.mybir as mybir
+from concourse.masks import make_identity
 
 F32 = mybir.dt.float32
 BF16 = mybir.dt.bfloat16
@@ -60,10 +61,12 @@ def tile_list_crater_degradation_ranker_kernel(
             return w1[PASS * a : PASS * (a + 1), c0:c1].rearrange("(p i) c -> p i c", i=PACK)
 
         tab_sc = held([P, T], U8, "tab_sc")
-        w2_sc_raw = held([P, 2, H], U8, "w2_sc_raw")
+        w2_sc_raw = held([P, H], U8, "w2_sc_raw")
+        w2_sc = held([P, 2, H], U8, "w2_sc")
         tab2_sc = held([P, T], U8, "tab2_sc")
         nc.vector.memset(tab_sc[:].bitcast(I32), 0)
-        nc.vector.memset(w2_sc_raw[:].rearrange("p a c -> p (a c)").bitcast(I32), 0)
+        nc.vector.memset(w2_sc_raw[:].bitcast(I32), 0)
+        nc.vector.memset(w2_sc[:].rearrange("p a c -> p (a c)").bitcast(I32), 0)
         nc.vector.memset(tab2_sc[:].bitcast(I32), 0)
         w1_raw = {}
 
@@ -71,6 +74,8 @@ def tile_list_crater_degradation_ranker_kernel(
             w1_raw[b, a] = held([P, PACK, PASS], F32, "w1_raw%d%d" % (b, a), tag="stage%d" % (2 * b + a))
             nc.sync.dma_start(w1_raw[b, a][:], w1_rows(a, PASS * b, PASS * (b + 1)))
 
+        wgs_rows = held([P, S], F32, "wgs_rows")
+        nc.sync.dma_start(wgs_rows[:], wgs)
         tabw = {0: load_words(tab_words, 0, "tabw0", parts=2)}
         idx = load_list(offs, "idx")
         tabw[1] = load_words(tab_words, 1, "tabw1")
@@ -80,11 +85,9 @@ def tile_list_crater_degradation_ranker_kernel(
         load_w1(0, 0)
         g_sb = held([P, 2, PACK], F32, "g_sb")
         nc.sync.dma_start(g_sb[:], gain.rearrange("(b p t) -> p b t", b=2, t=PACK))
-        for q in range(4):
-            nc.sync.dma_start(
-                w2_sc_raw[32 * q : 32 * q + 4, :, :].bitcast(I32),
-                w2_scales[:, 4 * q : 4 * q + 4, :].rearrange("a r c -> r a c").bitcast(I32),
-            )
+        nc.sync.dma_start(
+            w2_sc_raw[0:P:4, :].bitcast(I32), w2_scales.rearrange("a q c -> (a q) c").bitcast(I32)
+        )
         load_w1(0, 1)
         load_w1(1, 0)
         w1_last = []
@@ -92,9 +95,48 @@ def tile_list_crater_degradation_ranker_kernel(
             tile = held([P, PACK, PASS // 2], F32, "w1_last%d" % u)
             nc.sync.dma_start(tile[:], w1_rows(1, PASS + u * (PASS // 2), PASS + (u + 1) * (PASS // 2)))
             w1_last.append(tile)
+        ident = held([P, P], F32, "ident")
+        make_identity(nc, ident[:])
         wg = held([P, PACK, S], F32, "wg")
-        for q in (0, 2, 1, 3):
-            nc.sync.dma_start(wg[32 * q : 32 * q + 32, :, :], wgs.rearrange("(p t) j -> p t j", t=PACK))
+
+        turned = bank([P, 4, P], 0, "wgs_turned")
+        for jb in range(4):
+            nc.tensor.transpose(turned[:, jb, :], wgs_rows[:, P * jb : P * (jb + 1)], ident[:])
+        spread = held([P, 4, PACK, 4, 32], F32, "wgs_spread", tag="stage3")
+        nc.scalar.copy(
+            spread[:],
+            turned[:].rearrange("p b (m t) -> p b t m", t=PACK).unsqueeze(3).to_broadcast([P, 4, PACK, 4, 32]),
+        )
+        for t in range(PACK):
+            back = bank([P, 4, P], 4 + t, "wgs_back%d" % t)
+            for jb in range(4):
+                nc.tensor.transpose(back[:, jb, :], spread[:, jb, t].rearrange("p q m -> p (q m)"), ident[:])
+            nc.scalar.copy(wg[:, t, :], back[:].rearrange("p b j -> p (b j)"))
+
+        v_w = [held([P, S], U32, "v_w%d" % a) for a in range(2)]
+        v_sc = held([P, S], U8, "v_sc")
+        nc.vector.tensor_copy(v_w[0][:], tabw[0][:].indirect(idx[:]))
+        nc.vector.tensor_copy(v_sc[:], tab_sc[:].indirect(idx[:]))
+        nc.vector.tensor_copy(v_w[1][:], tabw[1][:].indirect(idx[:]))
+        m2g = held([P, 2, PACK], F32, "m2g")
+        nc.scalar.activation(m2g[:], g_sb[:], ACT.Copy, scale=-2.0)
+
+        w2_q = held([P, 4, PACK, P], U16, "w2_q")
+        nc.vector.tensor_copy(
+            w2_q[:].rearrange("p g t m -> p g m t"),
+            w2_raw[:].rearrange("p a c -> p (a c)").bitcast(U16).rearrange("p (g m t) -> p g m t", g=4, t=PACK),
+        )
+        w2_sc_dealt = held([P, 2, PACK, P], U8, "w2_sc_dealt")
+        nc.vector.tensor_copy(
+            w2_sc_dealt[:].rearrange("p b t m -> p b m t"),
+            w2_sc_raw[:].rearrange("p (b m t) -> p b m t", b=2, t=PACK),
+        )
+        for a in range(2):
+            for r in range(4):
+                nc.sync.dma_start(
+                    w2_sc[r:P:32, a, :].bitcast(I32),
+                    w2_sc_dealt[64 * a + 4 * r : 64 * (a + 1) : 16].rearrange("p b t m -> p (b t m)").bitcast(I32),
+                )
         idx3 = load_list(offs3, "idx3")
         page = {}
         base_sb = {}
@@ -118,14 +160,6 @@ def tile_list_crater_degradation_ranker_kernel(
         age_sb = held([P, S2 // P], F32, "age_sb")
         with nc.allow_non_contiguous_dma(reason="one age value per partition and tile"):
             nc.sync.dma_start(age_sb[:], age.rearrange("(m p) -> p m", p=P))
-
-        v_w = [held([P, S], U32, "v_w%d" % a) for a in range(2)]
-        v_sc = held([P, S], U8, "v_sc")
-        nc.vector.tensor_copy(v_w[0][:], tabw[0][:].indirect(idx[:]))
-        nc.vector.tensor_copy(v_sc[:], tab_sc[:].indirect(idx[:]))
-        nc.vector.tensor_copy(v_w[1][:], tabw[1][:].indirect(idx[:]))
-        m2g = held([P, 2, PACK], F32, "m2g")
-        nc.scalar.activation(m2g[:], g_sb[:], ACT.Copy, scale=-2.0)
 
         w1_q = {}
         w1_sc = {}
@@ -229,19 +263,6 @@ def tile_list_crater_degradation_ranker_kernel(
                     x_q[h, b][:, cols].bitcast(FP8X4), x_sc[h, b][:, cols], x_bf[:].rearrange("p j t -> p (j t)")
                 )
 
-        w2_q = held([P, 4, PACK, P], U16, "w2_q")
-        w2_sc = held([P, 4, PACK, P], U8, "w2_sc")
-
-        def deal_w2():
-            nc.vector.tensor_copy(
-                w2_q[:].rearrange("p g t m -> p g m t"),
-                w2_raw[:].rearrange("p a c -> p (a c)").bitcast(U16).rearrange("p (g m t) -> p g m t", g=4, t=PACK),
-            )
-            nc.vector.tensor_copy(
-                w2_sc[:].rearrange("p g t m -> p g m t"),
-                w2_sc_raw[:].rearrange("p a (b m t) -> p (a b) m t", b=2, t=PACK),
-            )
-
         y = {}
 
         def second_product(h):
@@ -256,7 +277,7 @@ def tile_list_crater_degradation_ranker_kernel(
                         nc.tensor.matmul_mx(
                             acc[b, t // 2][:, t % 2, :],
                             lhsT=w2_q[:, 2 * a + b, t, :].bitcast(FP4X4),
-                            lhsT_scale=w2_sc[:, 2 * a + b, t, :],
+                            lhsT_scale=w2_sc[:, a, PASS * b + P * t : PASS * b + P * (t + 1)],
                             rhs=x_q[h, a][:].bitcast(FP8X4),
                             rhs_scale=x_sc[h, a][:],
                             start=(a == 0 and t % 2 == 0), stop=(a == 1 and t % 2 == 1),
@@ -357,7 +378,6 @@ def tile_list_crater_degradation_ranker_kernel(
                 nc.scalar.activation(picked[m][:, 0, cols], picked[m][:, 1, cols], ACT.Copy, scale=age_sb[:, m : m + 1])
                 nc.sync.dma_start(out[P * m : P * (m + 1), cols], picked[m][:, 0, cols])
 
-        deal_w2()
         quantise_w1(0, 0)
         quantise_w1(0, 1)
         first_product(0, 0)

from contextlib import ExitStack

import concourse.mybir as mybir
from concourse.masks import make_identity

F32 = mybir.dt.float32
BF16 = mybir.dt.bfloat16
I32 = mybir.dt.int32
U32 = mybir.dt.uint32
U16 = mybir.dt.uint16
U8 = mybir.dt.uint8
FP8X4 = mybir.dt.float8_e4m3fn_x4
FP4X4 = mybir.dt.float4_e2m1fn_x4
ACT = mybir.ActivationFunctionType
ALU = mybir.AluOpType

P = 128
PACK = 4
PASS = P * PACK
K, T, S, H, T2, S2, NP = 1024, 2048, 512, 1024, 1024, 512, 512
HALF = S // 2
SCALAR_SHARE = 64
FLOPS = 2 * K * H * S + 2 * H * H * S + 2 * H * S2 * T2


def tile_list_crater_degradation_ranker_kernel(
    tc, tab_words, tab_scales, tab2_words, tab2_scales, w1, w2_words, w2_scales,
    gain, page0, wgs, base, age, offs, offs2, offs3, pos1, pos2, out,
):
    nc = tc.nc
    with ExitStack() as ctx:
        keep = ctx.enter_context(tc.tile_pool(name="keep", bufs=1))
        psum = ctx.enter_context(tc.psum_pool(name="psum", bufs=1))

        def held(shape, dtype, name, tag=None, bufs=1):
            return keep.tile(shape, dtype, name=name, tag=tag or name, bufs=bufs, align_bytes=64)

        def bank(shape, index, name):
            return psum.tile(shape, F32, name=name, tag="bank%d" % index)

        def load_list(src, name):
            tile = held([P, S // 16], U16, name)
            nc.sync.dma_start(tile[:], src)
            return tile

        def load_words(src, a, name, parts=1):
            tile = held([P, T], U32, name, tag="words", bufs=2)
            rows = src[a].rearrange("p t i -> p (t i)").bitcast(I32)
            for part in range(parts):
                cols = slice(T // parts * part, T // parts * (part + 1))
                nc.sync.dma_start(tile[:, cols].bitcast(I32), rows[:, cols])
            return tile

        def load_table_scales(queue, src, tile):
            for q in range(4):
                queue.dma_start(
                    tile[32 * q : 32 * q + 8, :].bitcast(I32), src[:, 4 * q : 4 * q + 4, :].bitcast(I32)
                )

        def w1_rows(a, c0, c1):
            return w1[PASS * a : PASS * (a + 1), c0:c1].rearrange("(p i) c -> p i c", i=PACK)

        tab_sc = held([P, T], U8, "tab_sc")
        w2_sc_raw = held([P, H], U8, "w2_sc_raw")
        w2_sc = held([P, 2, H], U8, "w2_sc")
        tab2_sc = held([P, T], U8, "tab2_sc")
        nc.vector.memset(tab_sc[:].bitcast(I32), 0)
        nc.vector.memset(w2_sc_raw[:].bitcast(I32), 0)
        nc.vector.memset(w2_sc[:].rearrange("p a c -> p (a c)").bitcast(I32), 0)
        nc.vector.memset(tab2_sc[:].bitcast(I32), 0)
        w1_raw = {}

        def load_w1(b, a):
            w1_raw[b, a] = held([P, PACK, PASS], F32, "w1_raw%d%d" % (b, a), tag="stage%d" % (2 * b + a))
            nc.sync.dma_start(w1_raw[b, a][:], w1_rows(a, PASS * b, PASS * (b + 1)))

        wgs_rows = held([P, S], F32, "wgs_rows")
        nc.sync.dma_start(wgs_rows[:], wgs)
        tabw = {0: load_words(tab_words, 0, "tabw0", parts=2)}
        idx = load_list(offs, "idx")
        tabw[1] = load_words(tab_words, 1, "tabw1")
        load_table_scales(nc.sync, tab_scales, tab_sc)
        w2_raw = held([P, 2, 2 * H], U8, "w2_raw")
        nc.sync.dma_start(w2_raw[:].bitcast(I32), w2_words.rearrange("a p c -> p a c").bitcast(I32))
        load_w1(0, 0)
        g_sb = held([P, 2, PACK], F32, "g_sb")
        nc.sync.dma_start(g_sb[:], gain.rearrange("(b p t) -> p b t", b=2, t=PACK))
        nc.sync.dma_start(
            w2_sc_raw[0:P:4, :].bitcast(I32), w2_scales.rearrange("a q c -> (a q) c").bitcast(I32)
        )
        load_w1(0, 1)
        load_w1(1, 0)
        w1_last = []
        for u in range(2):
            tile = held([P, PACK, PASS // 2], F32, "w1_last%d" % u)
            nc.sync.dma_start(tile[:], w1_rows(1, PASS + u * (PASS // 2), PASS + (u + 1) * (PASS // 2)))
            w1_last.append(tile)
        ident = held([P, P], F32, "ident")
        make_identity(nc, ident[:])
        wg = held([P, PACK, S], F32, "wg")

        turned = bank([P, 4, P], 0, "wgs_turned")
        for jb in range(4):
            nc.tensor.transpose(turned[:, jb, :], wgs_rows[:, P * jb : P * (jb + 1)], ident[:])
        spread = held([P, 4, PACK, 4, 32], F32, "wgs_spread", tag="stage3")
        nc.scalar.copy(
            spread[:],
            turned[:].rearrange("p b (m t) -> p b t m", t=PACK).unsqueeze(3).to_broadcast([P, 4, PACK, 4, 32]),
        )
        for t in range(PACK):
            back = bank([P, 4, P], 4 + t, "wgs_back%d" % t)
            for jb in range(4):
                nc.tensor.transpose(back[:, jb, :], spread[:, jb, t].rearrange("p q m -> p (q m)"), ident[:])
            nc.scalar.copy(wg[:, t, :], back[:].rearrange("p b j -> p (b j)"))

        v_w = [held([P, S], U32, "v_w%d" % a) for a in range(2)]
        v_sc = held([P, S], U8, "v_sc")
        nc.vector.tensor_copy(v_w[0][:], tabw[0][:].indirect(idx[:]))
        nc.vector.tensor_copy(v_sc[:], tab_sc[:].indirect(idx[:]))
        nc.vector.tensor_copy(v_w[1][:], tabw[1][:].indirect(idx[:]))
        m2g = held([P, 2, PACK], F32, "m2g")
        nc.scalar.activation(m2g[:], g_sb[:], ACT.Copy, scale=-2.0)

        w2_q = held([P, 4, PACK, P], U16, "w2_q")
        nc.vector.tensor_copy(
            w2_q[:].rearrange("p g t m -> p g m t"),
            w2_raw[:].rearrange("p a c -> p (a c)").bitcast(U16).rearrange("p (g m t) -> p g m t", g=4, t=PACK),
        )
        w2_sc_dealt = held([P, 2, PACK, P], U8, "w2_sc_dealt")
        nc.vector.tensor_copy(
            w2_sc_dealt[:].rearrange("p b t m -> p b m t"),
            w2_sc_raw[:].rearrange("p (b m t) -> p b m t", b=2, t=PACK),
        )
        for a in range(2):
            for r in range(4):
                nc.sync.dma_start(
                    w2_sc[r:P:32, a, :].bitcast(I32),
                    w2_sc_dealt[64 * a + 4 * r : 64 * (a + 1) : 16].rearrange("p b t m -> p (b t m)").bitcast(I32),
                )
        idx3 = load_list(offs3, "idx3")
        page = {}
        base_sb = {}
        for b in range(2):
            rows = slice(PASS * b, PASS * (b + 1))
            for t in range(PACK):
                page[b, t] = held([P, T2], F32, "page%d%d" % (b, t))
                nc.sync.dma_start(page[b, t][:], page0[rows, :].rearrange("(p t) n -> t p n", t=PACK)[t])
        base_rows = [base[PASS * b : PASS * (b + 1), :].rearrange("(p t) n -> p t n", t=PACK) for b in range(2)]
        for u in range(2):
            base_sb[0, u] = held([P, 2, T2], F32, "base0%d" % u, tag="stage%d" % (3 - u))
            nc.sync.dma_start(base_sb[0, u][:], base_rows[0][:, 2 * u : 2 * u + 2, :])
        for nh in range(2):
            base_sb[1, nh] = held([P, PACK, PASS], F32, "base1%d" % nh, tag="stage%d" % (1 - nh))
            nc.sync.dma_start(base_sb[1, nh][:], base_rows[1][:, :, PASS * nh : PASS * (nh + 1)])
        load_table_scales(nc.sync, tab2_scales, tab2_sc)
        idx2 = load_list(offs2, "idx2")
        tab2w = [load_words(tab2_words, a, "tab2w%d" % a) for a in range(2)]
        p1 = load_list(pos1, "p1")
        p2 = load_list(pos2, "p2")
        age_sb = held([P, S2 // P], F32, "age_sb")
        with nc.allow_non_contiguous_dma(reason="one age value per partition and tile"):
            nc.sync.dma_start(age_sb[:], age.rearrange("(m p) -> p m", p=P))

        w1_q = {}
        w1_sc = {}

        def deal_w1(copy, dst, raw, m0, m1):
            copy(
                dst[:, :, m0:m1, :].rearrange("p t m i -> p m i t"),
                raw.rearrange("p i (m t) -> p m i t", t=PACK),
            )

        def quantise_w1(b, a):
            dealt = held([P, PACK, P, PACK], BF16, "w1_bf%d%d" % (b, a), tag="bfb" if (b, a) == (0, 1) else "bfa")
            w1_q[b, a] = held([P, PASS], U32, "w1_q%d%d" % (b, a))
            w1_sc[b, a] = held([P, PASS], U8, "w1_sc%d%d" % (b, a))
            if (b, a) == (1, 1):
                for u in range(2):
                    deal_w1(nc.vector.tensor_copy, dealt, w1_last[u][:], u * (P // 2), (u + 1) * (P // 2))
                for t in range(PACK):
                    cols = slice(P * t, P * (t + 1))
                    nc.vector.quantize_mx(
                        w1_q[b, a][:, cols].bitcast(FP8X4), w1_sc[b, a][:, cols],
                        dealt[:, t, :, :].rearrange("p m i -> p (m i)"),
                    )
            else:
                m_scalar = {(0, 0): P, (0, 1): SCALAR_SHARE, (1, 0): 0}[b, a]
                if m_scalar > 0:
                    deal_w1(nc.scalar.copy, dealt, w1_raw[b, a][:, :, : PACK * m_scalar], 0, m_scalar)
                if m_scalar < P:
                    deal_w1(nc.vector.tensor_copy, dealt, w1_raw[b, a][:, :, PACK * m_scalar :], m_scalar, P)
                nc.vector.quantize_mx(
                    w1_q[b, a][:].bitcast(FP8X4), w1_sc[b, a][:], dealt[:].rearrange("p t m i -> p (t m i)")
                )

        z = {}

        def first_product(h, b):
            cols = slice(HALF * h, HALF * (h + 1))
            for u in range(2):
                z[h, b, u] = bank([P, 2, HALF], 2 * (h + b) + u, "z%d%d%d" % (h, b, u))
            for a in range(2):
                for t in range(PACK):
                    nc.tensor.matmul_mx(
                        z[h, b, t // 2][:, t % 2, :],
                        lhsT=w1_q[b, a][:, P * t : P * (t + 1)].bitcast(FP8X4),
                        lhsT_scale=w1_sc[b, a][:, P * t : P * (t + 1)],
                        rhs=v_w[a][:, cols].bitcast(FP8X4),
                        rhs_scale=v_sc[4 * a : P, cols],
                        start=(a == 0 and t % 2 == 0), stop=(a == 1 and t % 2 == 1),
                    )

        x = {}
        x_q = {}
        x_sc = {}

        def cosine(h, b):
            if (h, b) == (1, 0):
                sines = held([P, PACK, HALF], F32, "sines10", tag="x", bufs=4)
                tile = held([P, PACK, HALF], F32, "x10", tag="c2")
            else:
                tile = held([P, PACK, HALF], F32, "x%d%d" % (h, b), tag="x", bufs=4)
                sines = tile
            x[h, b] = tile
            for u in range(2):
                nc.scalar.activation(sines[:, 2 * u : 2 * u + 2, :], z[h, b, u][:], ACT.Sin, scale=0.5)
            split = (h, b) == (0, 1)
            for u in range(1 if split else 0, 2):
                nc.scalar.activation(tile[:, 2 * u : 2 * u + 2, :], sines[:, 2 * u : 2 * u + 2, :], ACT.Square)
            for t in range(PACK):
                if split and t < 2:
                    nc.vector.scalar_tensor_tensor(
                        tile[:, t, :], tile[:, t, :], m2g[:, b, t : t + 1], tile[:, t, :], ALU.mult, ALU.mult
                    )
            for t in range(PACK):
                if split and t < 2:
                    nc.vector.tensor_scalar(tile[:, t, :], tile[:, t, :], g_sb[:, b, t : t + 1], None, ALU.add)
                elif split:
                    nc.vector.tensor_scalar(
                        tile[:, t, :], tile[:, t, :], m2g[:, b, t : t + 1], g_sb[:, b, t : t + 1], ALU.mult, ALU.add
                    )
                else:
                    nc.scalar.activation(
                        tile[:, t, :], tile[:, t, :], ACT.Identity,
                        bias=g_sb[:, b, t : t + 1], scale=m2g[:, b, t : t + 1],
                    )
            x_q[h, b] = held([P, HALF], U32, "x_q%d%d" % (h, b))
            x_sc[h, b] = held([P, HALF], U8, "x_sc%d%d" % (h, b))
            tags = {(0, 0): ["bfa"], (0, 1): ["c1", "c2"], (1, 0): [None], (1, 1): ["mid"]}[h, b]
            width = HALF // len(tags)
            copy = nc.vector.tensor_copy if h == 0 else nc.scalar.copy
            woven = []
            for part, tag in enumerate(tags):
                x_bf = held([P, width, PACK], BF16, "x_bf%d%d%d" % (h, b, part), tag=tag)
                copy(
                    x_bf[:].rearrange("p (c i) t -> p c t i", i=4),
                    tile[:, :, width * part : width * (part + 1)].rearrange("p t (c i) -> p c t i", i=4),
                )
                woven.append(x_bf)
            for part, x_bf in enumerate(woven):
                cols = slice(width * part, width * (part + 1))
                nc.vector.quantize_mx(
                    x_q[h, b][:, cols].bitcast(FP8X4), x_sc[h, b][:, cols], x_bf[:].rearrange("p j t -> p (j t)")
                )

        y = {}

        def second_product(h):
            acc = {}
            for b in range(2):
                y[h, b] = held([P, PACK, HALF], F32, "y%d%d" % (h, b), tag="y", bufs=4)
                for u in range(2):
                    acc[b, u] = bank([P, 2, HALF], 4 * (1 - h) + 2 * b + u, "y_ps%d%d%d" % (h, b, u))
            for a in range(2):
                for b in range(2):
                    for t in range(PACK):
                        nc.tensor.matmul_mx(
                            acc[b, t // 2][:, t % 2, :],
                            lhsT=w2_q[:, 2 * a + b, t, :].bitcast(FP4X4),
                            lhsT_scale=w2_sc[:, a, PASS * b + P * t : PASS * b + P * (t + 1)],
                            rhs=x_q[h, a][:].bitcast(FP8X4),
                            rhs_scale=x_sc[h, a][:],
                            start=(a == 0 and t % 2 == 0), stop=(a == 1 and t % 2 == 1),
                        )
            for b in range(2):
                for u in range(2):
                    nc.scalar.copy(y[h, b][:, 2 * u : 2 * u + 2, :], acc[b, u][:])

        def place(h, b):
            tags = {(0, 0): ["c1"], (0, 1): ["c1", "mid"], (1, 0): [None], (1, 1): ["stage2"]}[h, b]
            rows = PACK // len(tags)
            for part, tag in enumerate(tags):
                ts = slice(rows * part, rows * (part + 1))
                xw = held([P, rows, HALF], F32, "xw%d%d%d" % (h, b, part), tag=tag)
                nc.vector.tensor_tensor(xw[:], x[h, b][:, ts, :], wg[:, ts, HALF * h : HALF * (h + 1)], ALU.mult)
                for e in range(rows):
                    t = rows * part + e
                    nc.vector.tensor_tensor(
                        page[b, t][:].indirect(idx3[:, 16 * h : 16 * (h + 1)]), xw[:, e, :], y[h, b][:, t, :], ALU.mult
                    )

        top_q = {}
        top_sc = {}

        def weave_and_quantise(b, top, src_cols, dst_cols, name, tag, bufs):
            width = dst_cols.stop - dst_cols.start
            woven = held([P, width, PACK], BF16, name, tag=tag, bufs=bufs)
            nc.scalar.copy(
                woven[:].rearrange("p (c i) t -> p c t i", i=4),
                top[:, :, src_cols].rearrange("p t (c i) -> p c t i", i=4),
            )
            nc.vector.quantize_mx(
                top_q[b][:, dst_cols].bitcast(FP8X4), top_sc[b][:, dst_cols], woven[:].rearrange("p n t -> p (n t)")
            )

        def raise_to_base(b):
            top_q[b] = held([P, T2], U32, "top_q%d" % b)
            top_sc[b] = held([P, T2], U8, "top_sc%d" % b)
            if b == 0:
                top = held([P, PACK, T2], BF16, "top0")
                for t in range(PACK):
                    nc.vector.tensor_tensor(top[:, t, :], page[b, t][:], base_sb[b, t // 2][:, t % 2, :], ALU.max)
                weave_and_quantise(b, top, slice(0, T2), slice(0, T2), "woven0", None, 1)
                return
            width = PASS // 2
            for nh in range(2):
                top = held([P, PACK, PASS], BF16, "top1%d" % nh, tag="top", bufs=2)
                for t in range(PACK):
                    nc.vector.tensor_tensor(
                        top[:, t, :], page[b, t][:, PASS * nh : PASS * (nh + 1)], base_sb[b, nh][:, t, :], ALU.max
                    )
                for part in range(2):
                    last = (nh, part) == (1, 1)
                    c0 = width * part
                    weave_and_quantise(
                        b, top, slice(c0, c0 + width), slice(PASS * nh + c0, PASS * nh + c0 + width),
                        "woven1%d%d" % (nh, part), "late" if last else "x", 1 if last else 4,
                    )

        def candidates(mh):
            words = held([P, 2, HALF], U32, "v2_w%d" % mh, tag="late" if mh == 1 else "stage1")
            scales = held([P, HALF], U8, "v2_sc%d" % mh, tag="stage0" if mh == 1 else "stage2")
            entries = idx2[:, 16 * mh : 16 * (mh + 1)]
            nc.vector.tensor_copy(scales[:], tab2_sc[:].indirect(entries))
            for a in range(2):
                nc.vector.tensor_copy(words[:, a, :], tab2w[a][:].indirect(entries))
            return words, scales

        def scores(m, words, scales):
            cols = slice(P * (m % 2), P * (m % 2 + 1))
            e_sb = held([P, T2], F32, "e%d" % m, tag="y", bufs=4)
            for nh in range(2):
                acc = bank([P, PASS], (6, 4, 0, 2)[m] + nh, "e_ps%d%d" % (m, nh))
                n_cols = slice(PASS * nh, PASS * (nh + 1))
                for a in range(2):
                    nc.tensor.matmul_mx(
                        acc[:],
                        lhsT=words[:, a, cols].bitcast(FP8X4), lhsT_scale=scales[4 * a : P, cols],
                        rhs=top_q[a][:, n_cols].bitcast(FP8X4), rhs_scale=top_sc[a][:, n_cols],
                        start=(a == 0), stop=(a == 1),
                    )
                nc.scalar.copy(e_sb[:, n_cols], acc[:])
            return e_sb

        picked = {}

        def pick_first(m, e_sb):
            picked[m] = held([P, 2, NP], F32, "picked%d" % m, tag="x", bufs=4)
            nc.vector.tensor_copy(picked[m][:, 0, :], e_sb[:].indirect(p1[:]))

        def add_second(m, e_sb):
            edges = (0, 384, NP) if m == 3 else (0, NP)
            for c0, c1 in zip(edges[:-1], edges[1:]):
                cols = slice(c0, c1)
                nc.vector.tensor_tensor(
                    picked[m][:, 1, cols], e_sb[:].indirect(p2[:, c0 // 16 : c1 // 16]), picked[m][:, 0, cols], ALU.add
                )
                nc.scalar.activation(picked[m][:, 0, cols], picked[m][:, 1, cols], ACT.Copy, scale=age_sb[:, m : m + 1])
                nc.sync.dma_start(out[P * m : P * (m + 1), cols], picked[m][:, 0, cols])

        quantise_w1(0, 0)
        quantise_w1(0, 1)
        first_product(0, 0)
        quantise_w1(1, 0)
        quantise_w1(1, 1)
        cosine(0, 0)
        first_product(0, 1)
        cosine(0, 1)
        second_product(0)
        first_product(1, 0)
        first_product(1, 1)
        cosine(1, 0)
        cosine(1, 1)
        second_product(1)
        place(0, 0)
        place(0, 1)
        place(1, 0)
        raise_to_base(0)
        place(1, 1)
        raise_to_base(1)
        first = candidates(0)
        e_low = [scores(m, *first) for m in range(2)]
        second = candidates(1)
        e_high = [scores(m, *second) for m in range(2, 4)]
        e_all = e_low + e_high
        pick_first(0, e_all[0])
        for m in range(4):
            if m < 3:
                pick_first(m + 1, e_all[m + 1])
            add_second(m, e_all[m])
